import numpy as np
import ml_dtypes


def mxq(x, axis, fmt="e4m3"):
    dtype, down = {"e4m3": (ml_dtypes.float8_e4m3fn, 7), "e5m2": (ml_dtypes.float8_e5m2, 14)}[fmt]
    v = np.moveaxis(np.asarray(x, np.float32).astype(ml_dtypes.bfloat16).astype(np.float64), axis, -1)
    blocks = v.reshape(v.shape[:-1] + (-1, 32))
    amax = np.abs(blocks).max(-1, keepdims=True)
    byte = np.maximum(np.where(amax > 0, np.frexp(amax)[1] - 1 + 127, 0) - down, 1)
    scale = np.exp2(byte - 127.0)
    codes = (blocks / scale).astype(np.float32).astype(dtype).astype(np.float64)
    return np.moveaxis((codes * scale).reshape(v.shape), -1, axis)


WIDE = False


def mx_kscale(k):
    if not WIDE:
        return np.ones(k)
    levels = np.array([10, -10, 5, -5, 0])
    if k % 512:
        return np.exp2(np.random.permutation(np.resize(levels, k // 32))).repeat(32)
    a = np.empty((k // 512, 16))
    for p in range(k // 512):
        a[p, :8] = np.random.permutation(np.resize(levels, 8))
        for g in range(8):
            far = levels[np.abs(levels - a[p, g]) >= 10]
            a[p, g + 8] = far[np.random.randint(len(far))]
    return np.exp2(a.ravel()).repeat(32)


def f64(x):
    return np.asarray(x).astype(np.float64)


def striped(idx):
    return np.tile(np.asarray(idx).reshape(-1, 16).T, (8, 1)).astype(np.uint16)


def unstriped(offs):
    return offs[:16].T.reshape(-1).astype(np.int64)


E2M1 = np.array([0.0, 0.5, 1.0, 1.5, 2.0, 3.0, 4.0, 6.0, -0.0, -0.5, -1.0, -1.5, -2.0, -3.0, -4.0, -6.0])


def pack_weight(w, fmt):
    k, n = w.shape
    w = f64(np.asarray(w, np.float32).astype(ml_dtypes.bfloat16)).reshape(k // 32, 32, n)
    amax = np.abs(w).max(1)
    if fmt == "e4m3":
        byte = np.frexp(amax)[1] - 1 + 127 - 7
    else:
        mant, ex = np.frexp(amax / 6.0)
        byte = np.where(mant > 0.5, ex, ex - 1) + 127
    byte = np.clip(np.where(amax > 0, byte, 1), 1, 254)
    scaled = (w * np.exp2(127.0 - byte)[:, None, :]).reshape(k, n).astype(np.float32)
    by_word = np.ascontiguousarray(scaled.reshape(k // 512, 128, 4, n).transpose(0, 1, 3, 2))
    if fmt == "e4m3":
        words = by_word.astype(ml_dtypes.float8_e4m3fn).view(np.uint8)
    else:
        c = by_word.astype(ml_dtypes.float4_e2m1fn).view(np.uint8) & 0xF
        words = (c[..., 0::2] | (c[..., 1::2] << 4)).reshape(k // 512, 128, 2 * n)
    return np.ascontiguousarray(words), np.ascontiguousarray(byte.astype(np.uint8).reshape(k // 512, 16, n))


def unpack_weight(words, scales, fmt):
    g, _, n = scales.shape
    words = np.ascontiguousarray(words).reshape(g, 128, n, -1)
    if fmt == "e4m3":
        vals = words.view(ml_dtypes.float8_e4m3fn).astype(np.float64)
    else:
        nib = np.empty((g, 128, n, 4), np.uint8)
        nib[..., 0::2] = words & 0xF
        nib[..., 1::2] = words >> 4
        vals = E2M1[nib]
    vals = vals * np.repeat(np.exp2(scales.astype(np.float64) - 127.0), 8, axis=1)[..., None]
    return vals.transpose(0, 1, 3, 2).reshape(g * 512, n)


D, K, R, T, I, Q, G = 512, 512, 512, 2048, 512, 128, 32


def setup_inputs():
    n = np.random.standard_normal
    idx = np.random.permutation(T)[:I]
    fd = mx_kscale(D)
    fk = mx_kscale(K)
    fi = mx_kscale(I)
    keysp = pack_weight(n((D, T)) / fd[:, None], "e2m1")
    tabp = pack_weight(n((K, T)) / fk[:, None], "e2m1")
    return {
        "query": (n((D, Q)) * 0.7 / np.sqrt(D) * fd[:, None]).astype(np.float32),
        "keys_words": keysp[0],
        "keys_scales": keysp[1],
        "tab_words": tabp[0],
        "tab_scales": tabp[1],
        "w1": (n((K, R)) * 1 / np.sqrt(K) * fk[:, None]).astype(np.float32),
        "share": (np.random.uniform(0.4, 1.0, (R, 1))).astype(np.float32),
        "os": (np.random.uniform(4.0, 16.0, (1, I)) * fi).astype(np.float32),
        "vs": (np.random.uniform(0.5, 2.0, (1, I)) / fi).astype(np.float32),
        "offs": striped(idx),
    }


def reference(query, keys_words, keys_scales, tab_words, tab_scales, w1, share, os, vs, offs):
    idx = unstriped(offs)
    keysu = unpack_weight(keys_words, keys_scales, "e2m1")
    tabu = unpack_weight(tab_words, tab_scales, "e2m1")
    queryq = mxq(f64(query), 0, "e4m3")
    keysidxg = keysu[:, idx]
    a = queryq.T @ keysidxg
    p = np.exp(a - np.max(a, axis=1, keepdims=True))
    z = np.sum(p, axis=1, keepdims=True)
    w = p / z
    w1q = mxq(f64(w1), 0, "e4m3")
    tabidxg = tabu[:, idx]
    zh = w1q.T @ tabidxg
    mz = zh.reshape(R, G, I // G).mean(axis=2)
    mzr = np.repeat(mz, I // G, axis=1)
    hv = np.tanh(zh - mzr * f64(share))
    wo1 = w * f64(os)
    wt1 = wo1.T
    hw = hv * f64(vs)
    ht1 = hw.T
    wt1q = mxq(wt1, 0, "e4m3")
    ht1q = mxq(ht1, 0, "e4m3")
    o = wt1q.T @ ht1q
    return o

@@ -1,0 +1,162 @@
+from contextlib import ExitStack
+
+import concourse.mybir as mybir
+from concourse.masks import make_identity
+
+D, K, R, T, I, Q, G = 512, 512, 512, 2048, 512, 128, 32
+FLOPS = 2 * (D * Q * I + K * R * I + I * Q * R)
+
+F32 = mybir.dt.float32
+BF16 = mybir.dt.bfloat16
+I32 = mybir.dt.int32
+U32 = mybir.dt.uint32
+U16 = mybir.dt.uint16
+U8 = mybir.dt.uint8
+FP8X4 = mybir.dt.float8_e4m3fn_x4
+FP4X4 = mybir.dt.float4_e2m1fn_x4
+ALU = mybir.AluOpType
+ACT = mybir.ActivationFunctionType
+AXIS = mybir.AxisListType
+
+P = 128
+PACK = 4
+PAGE = I // G
+CHUNKS = R // P
+
+
+def tile_attend_lrcentred_soft_kernel(tc, query, keys_words, keys_scales, tab_words, tab_scales, w1, share, slot_factor, value_scale, offs, out):
+    nc = tc.nc
+    with ExitStack() as ctx:
+        sb = ctx.enter_context(tc.tile_pool(name="sb", bufs=1))
+        ps = ctx.enter_context(tc.psum_pool(name="ps", bufs=1))
+
+        def sbuf(name, shape, dtype):
+            return sb.tile(shape, dtype, name=name, align_bytes=64)
+
+        def load_scale_rows(queue, plane, rows):
+            for quad in range(4):
+                queue.dma_start(out=plane[32 * quad : 32 * quad + 4, :].bitcast(I32), in_=rows[0, 4 * quad : 4 * quad + 4, :].bitcast(I32))
+
+        def gather(name, window, dtype):
+            picked = sbuf(name, [P, I], dtype)
+            nc.vector.tensor_copy(out=picked[:], in_=window[:].indirect(offsets[:]))
+            return picked
+
+        def quantize(name, grouped, width):
+            codes = sbuf(name + "_codes", [P, width], U32)
+            scales = sbuf(name + "_scales", [P, width], U8)
+            nc.vector.quantize_mx(out=codes[:].bitcast(FP8X4), scales=scales[:], in_=grouped[:].rearrange("p c j -> p (c j)"))
+            return codes, scales
+
+        def round_and_group(name, rows):
+            grouped = sbuf(name, [P, P, PACK], BF16)
+            nc.scalar.activation(out=grouped[:].rearrange("p (c i) j -> p c j i", i=4), in_=rows.rearrange("p j (c i) -> p c j i", i=4), func=ACT.Copy)
+            return grouped
+
+        offsets = sb.tile([P, I // 16], U16, name="offsets")
+        tab_plane = sbuf("tab_plane", [P, T], U8)
+        keys_plane = sbuf("keys_plane", [P, T], U8)
+        nc.vector.memset(tab_plane[:].bitcast(I32), 0)
+        nc.vector.memset(keys_plane[:].bitcast(I32), 0)
+
+        nc.sync.dma_start(offsets[:], offs)
+        tab_pool = sbuf("tab_pool", [P, T], U16)
+        nc.sync.dma_start(out=tab_pool[:].bitcast(I32), in_=tab_words[0].bitcast(I32))
+        load_scale_rows(nc.sync, tab_plane, tab_scales)
+
+        w1_rows = w1.rearrange("(p j) r -> p j r", j=PACK)
+        w1_raw = [sbuf(f"w1_raw{h}", [P, PACK, R // 2], F32) for h in range(2)]
+        keys_pool = sbuf("keys_pool", [P, T], U16)
+        q_raw = sbuf("q_raw", [P, PACK, Q], F32)
+        nc.sync.dma_start(out=w1_raw[0][:], in_=w1_rows[:, :, : R // 2])
+        nc.sync.dma_start(out=w1_raw[1][:], in_=w1_rows[:, :, R // 2 :])
+        nc.sync.dma_start(out=keys_pool[:].bitcast(I32), in_=keys_words[0].bitcast(I32))
+        load_scale_rows(nc.sync, keys_plane, keys_scales)
+        nc.sync.dma_start(out=q_raw[:], in_=query.rearrange("(p j) q -> p j q", j=PACK))
+
+        share_col = sbuf("share_col", [P, CHUNKS], F32)
+        vs_col = sbuf("vs_col", [P, PACK], F32)
+        os_col = sbuf("os_col", [P, PACK], F32)
+        with nc.allow_non_contiguous_dma(reason="one value of share to a partition and chunk"):
+            nc.gpsimd.dma_start(out=share_col[:], in_=share.rearrange("(c p) o -> p (c o)", p=P))
+        nc.gpsimd.dma_start(out=vs_col[:], in_=value_scale.rearrange("o (p j) -> (o p) j", j=PACK))
+        nc.gpsimd.dma_start(out=os_col[:], in_=slot_factor.rearrange("o (p j) -> (o p) j", j=PACK))
+        ident = sbuf("ident", [P, P], F32)
+        make_identity(nc, ident[:])
+        centre = sbuf("centre", [P, CHUNKS], F32)
+        nc.gpsimd.tensor_scalar(out=centre[:], in0=share_col[:], scalar1=-1.0 / PAGE, scalar2=0.0, op0=ALU.mult, op1=ALU.add)
+
+        tab_codes = gather("tab_codes", tab_pool, U16)
+        tab_bytes = gather("tab_bytes", tab_plane, U8)
+
+        layer = []
+        for c in range(CHUNKS):
+            half, part = divmod(c, 2)
+            grouped = round_and_group(f"w1_bf{c}", w1_raw[half][:, :, part * P : (part + 1) * P])
+            codes, scales = quantize(f"w1q{c}", grouped, P)
+            bank = ps.tile([P, I], F32, name=f"zh{c}", tag=f"zh{c}")
+            nc.tensor.matmul_mx(out=bank[:], lhsT=codes[:].bitcast(FP8X4), lhsT_scale=scales[:], rhs=tab_codes[:].bitcast(FP4X4), rhs_scale=tab_bytes[:], start=True, stop=True)
+            layer.append(bank)
+
+        def centre_chunk(c):
+            bank = layer[c]
+            page_sum = sbuf(f"page_sum{c}", [P, G], F32)
+            nc.vector.tensor_reduce(out=page_sum[:], in_=bank[:].rearrange("r (g s) -> r g s", s=PAGE), axis=AXIS.X, op=ALU.add)
+            shift = sbuf(f"shift{c}", [P, G, P // G], F32)
+            nc.scalar.activation(out=shift[:], in_=page_sum[:].unsqueeze(2).to_broadcast([P, G, P // G]), func=ACT.Copy, scale=centre[:, c : c + 1])
+            zh = sbuf(f"zh_sb{c}", [P, PACK, P], F32)
+            nc.scalar.copy(out=zh[:], in_=bank[:].rearrange("r (p j) -> r j p", j=PACK))
+            turned = ps.tile([P, PACK, P], F32, name="turned", tag="turned", bufs=2)
+            shift_flat = shift[:].rearrange("r g a -> r (g a)")
+            for j in range(PACK):
+                nc.tensor.matmul(out=turned[:, j, :], lhsT=shift_flat, rhs=ident[:], start=(j == 0), stop=False, is_transpose=True)
+            for j in range(PACK):
+                nc.tensor.matmul(out=turned[:, j, :], lhsT=zh[:, j, :], rhs=ident[:], start=False, stop=(j == PACK - 1), is_transpose=True)
+            return turned
+
+        def finish_chunk(c, turned):
+            hv = sbuf(f"hv{c}", [P, P, PACK], F32)
+            nc.scalar.activation(out=hv[:], in_=turned[:].rearrange("p j r -> p r j"), func=ACT.Tanh)
+            hw = sbuf(f"hw{c}", [P, P, PACK], BF16)
+            nc.vector.tensor_tensor(out=hw[:], in0=hv[:], in1=vs_col[:].unsqueeze(1).to_broadcast([P, P, PACK]), op=ALU.mult)
+            return quantize(f"h{c}", hw, P)
+
+        turned0 = centre_chunk(0)
+        turned1 = centre_chunk(1)
+
+        keys_codes = gather("keys_codes", keys_pool, U16)
+        keys_bytes = gather("keys_bytes", keys_plane, U8)
+        q_codes, q_scales = quantize("q", round_and_group("q_bf", q_raw[:]), Q)
+        scores = ps.tile([P, I], F32, name="scores", tag="scores")
+        nc.tensor.matmul_mx(out=scores[:], lhsT=q_codes[:].bitcast(FP8X4), lhsT_scale=q_scales[:], rhs=keys_codes[:].bitcast(FP4X4), rhs_scale=keys_bytes[:], start=True, stop=True)
+
+        hq = [finish_chunk(0, turned0)]
+        turned2 = centre_chunk(2)
+        neg_max = sbuf("neg_max", [P, 1], F32)
+        nc.vector.tensor_reduce(out=neg_max[:], in_=scores[:], axis=AXIS.X, op=ALU.max, negate=True)
+        hq.append(finish_chunk(1, turned1))
+        turned3 = centre_chunk(3)
+
+        expo = sbuf("expo", [P, PACK, P], F32)
+        row_sum = sbuf("row_sum", [P, 1], F32)
+        nc.scalar.activation(out=expo[:], in_=scores[:].rearrange("q (p j) -> q j p", j=PACK), func=ACT.Exp, bias=neg_max[:], accum_out=row_sum[:])
+        inv_sum = sbuf("inv_sum", [P, 1], F32)
+        nc.vector.reciprocal(out=inv_sum[:], in_=row_sum[:])
+        weights = sbuf("weights", [P, PACK, P], F32)
+        nc.scalar.activation(out=weights[:], in_=expo[:], func=ACT.Copy, scale=inv_sum[:])
+        w_turned = ps.tile([P, PACK, Q], F32, name="w_turned", tag="w_turned")
+        for j in range(PACK):
+            nc.tensor.transpose(w_turned[:, j, :], weights[:, j, :], ident[:])
+        hq.append(finish_chunk(2, turned2))
+        wt = sbuf("wt", [P, Q, PACK], BF16)
+        nc.vector.tensor_tensor(out=wt[:], in0=w_turned[:].rearrange("p j q -> p q j"), in1=os_col[:].unsqueeze(1).to_broadcast([P, Q, PACK]), op=ALU.mult)
+        w_codes, w_scales = quantize("w", wt, Q)
+        hq.append(finish_chunk(3, turned3))
+
+        for c in range(CHUNKS):
+            codes, scales = hq[c]
+            acc = ps.tile([P, P], F32, name=f"acc{c}", tag=f"zh{c}")
+            nc.tensor.matmul_mx(out=acc[:], lhsT=w_codes[:].bitcast(FP8X4), lhsT_scale=w_scales[:], rhs=codes[:].bitcast(FP8X4), rhs_scale=scales[:], start=True, stop=True)
+            result = sbuf(f"result{c}", [P, P], F32)
+            nc.scalar.copy(out=result[:], in_=acc[:])
+            nc.sync.dma_start(out=out[:, c * P : (c + 1) * P], in_=result[:])

@@ -28,10 +28,11 @@ def tile_attend_lrcentred_soft_kernel(tc, query, keys_words, keys_scales, tab_wo
     nc = tc.nc
     with ExitStack() as ctx:
         sb = ctx.enter_context(tc.tile_pool(name="sb", bufs=1))
+        reused = ctx.enter_context(tc.tile_pool(name="reused", bufs=1))
         ps = ctx.enter_context(tc.psum_pool(name="ps", bufs=1))
 
-        def sbuf(name, shape, dtype):
-            return sb.tile(shape, dtype, name=name, align_bytes=64)
+        def sbuf(name, shape, dtype, tag=None):
+            return sb.tile(shape, dtype, name=name, tag=tag or name, align_bytes=64)
 
         def load_scale_rows(queue, plane, rows):
             for quad in range(4):
@@ -48,14 +49,12 @@ def tile_attend_lrcentred_soft_kernel(tc, query, keys_words, keys_scales, tab_wo
             nc.vector.quantize_mx(out=codes[:].bitcast(FP8X4), scales=scales[:], in_=grouped[:].rearrange("p c j -> p (c j)"))
             return codes, scales
 
-        def round_and_group(name, rows):
-            grouped = sbuf(name, [P, P, PACK], BF16)
-            nc.scalar.activation(out=grouped[:].rearrange("p (c i) j -> p c j i", i=4), in_=rows.rearrange("p j (c i) -> p c j i", i=4), func=ACT.Copy)
-            return grouped
+        def round_and_group(grouped, rows):
+            nc.scalar.activation(out=grouped.rearrange("p (c i) j -> p c j i", i=4), in_=rows.rearrange("p j (c i) -> p c j i", i=4), func=ACT.Copy)
 
         offsets = sb.tile([P, I // 16], U16, name="offsets")
         tab_plane = sbuf("tab_plane", [P, T], U8)
-        keys_plane = sbuf("keys_plane", [P, T], U8)
+        keys_plane = reused.tile([P, T], U8, name="keys_plane", align_bytes=64, offset=0)
         nc.vector.memset(tab_plane[:].bitcast(I32), 0)
         nc.vector.memset(keys_plane[:].bitcast(I32), 0)
 
@@ -70,43 +69,41 @@ def tile_attend_lrcentred_soft_kernel(tc, query, keys_words, keys_scales, tab_wo
         q_raw = sbuf("q_raw", [P, PACK, Q], F32)
         nc.sync.dma_start(out=w1_raw[0][:], in_=w1_rows[:, :, : R // 2])
         nc.sync.dma_start(out=w1_raw[1][:], in_=w1_rows[:, :, R // 2 :])
-        nc.sync.dma_start(out=keys_pool[:].bitcast(I32), in_=keys_words[0].bitcast(I32))
         load_scale_rows(nc.sync, keys_plane, keys_scales)
         nc.sync.dma_start(out=q_raw[:], in_=query.rearrange("(p j) q -> p j q", j=PACK))
+        nc.sync.dma_start(out=keys_pool[:].bitcast(I32), in_=keys_words[0].bitcast(I32))
 
-        share_col = sbuf("share_col", [P, CHUNKS], F32)
+        share_rows = sbuf("share_rows", [P, P], F32)
+        nc.gpsimd.memset(share_rows[:], 0.0)
+        nc.scalar.dma_start(out=share_rows[:CHUNKS, :], in_=share.rearrange("(c p) o -> c (p o)", p=P))
         vs_col = sbuf("vs_col", [P, PACK], F32)
         os_col = sbuf("os_col", [P, PACK], F32)
-        with nc.allow_non_contiguous_dma(reason="one value of share to a partition and chunk"):
-            nc.gpsimd.dma_start(out=share_col[:], in_=share.rearrange("(c p) o -> p (c o)", p=P))
-        nc.gpsimd.dma_start(out=vs_col[:], in_=value_scale.rearrange("o (p j) -> (o p) j", j=PACK))
-        nc.gpsimd.dma_start(out=os_col[:], in_=slot_factor.rearrange("o (p j) -> (o p) j", j=PACK))
+        nc.sync.dma_start(out=vs_col[:], in_=value_scale.rearrange("o (p j) -> (o p) j", j=PACK))
+        nc.sync.dma_start(out=os_col[:], in_=slot_factor.rearrange("o (p j) -> (o p) j", j=PACK))
         ident = sbuf("ident", [P, P], F32)
         make_identity(nc, ident[:])
         centre = sbuf("centre", [P, CHUNKS], F32)
-        nc.gpsimd.tensor_scalar(out=centre[:], in0=share_col[:], scalar1=-1.0 / PAGE, scalar2=0.0, op0=ALU.mult, op1=ALU.add)
+        share_turned = ps.tile([P, P], F32, name="share_turned", tag="w_turned")
+        nc.tensor.transpose(share_turned[:], share_rows[:], ident[:])
+        nc.vector.tensor_scalar(out=centre[:], in0=share_turned[:, :CHUNKS], scalar1=-1.0 / PAGE, scalar2=None, op0=ALU.mult)
 
         tab_codes = gather("tab_codes", tab_pool, U16)
         tab_bytes = gather("tab_bytes", tab_plane, U8)
 
-        layer = []
-        for c in range(CHUNKS):
-            half, part = divmod(c, 2)
-            grouped = round_and_group(f"w1_bf{c}", w1_raw[half][:, :, part * P : (part + 1) * P])
-            codes, scales = quantize(f"w1q{c}", grouped, P)
+        def layer_product(c, codes, scales):
             bank = ps.tile([P, I], F32, name=f"zh{c}", tag=f"zh{c}")
-            nc.tensor.matmul_mx(out=bank[:], lhsT=codes[:].bitcast(FP8X4), lhsT_scale=scales[:], rhs=tab_codes[:].bitcast(FP4X4), rhs_scale=tab_bytes[:], start=True, stop=True)
-            layer.append(bank)
+            nc.tensor.matmul_mx(out=bank[:], lhsT=codes.bitcast(FP8X4), lhsT_scale=scales, rhs=tab_codes[:].bitcast(FP4X4), rhs_scale=tab_bytes[:], start=True, stop=True)
+            return bank
 
         def centre_chunk(c):
             bank = layer[c]
-            page_sum = sbuf(f"page_sum{c}", [P, G], F32)
-            nc.vector.tensor_reduce(out=page_sum[:], in_=bank[:].rearrange("r (g s) -> r g s", s=PAGE), axis=AXIS.X, op=ALU.add)
+            page_sum = page_sums[:, c * G : (c + 1) * G]
+            nc.vector.tensor_reduce(out=page_sum, in_=bank[:].rearrange("r (g s) -> r g s", s=PAGE), axis=AXIS.X, op=ALU.add)
             shift = sbuf(f"shift{c}", [P, G, P // G], F32)
-            nc.scalar.activation(out=shift[:], in_=page_sum[:].unsqueeze(2).to_broadcast([P, G, P // G]), func=ACT.Copy, scale=centre[:, c : c + 1])
+            nc.scalar.activation(out=shift[:], in_=page_sum.unsqueeze(2).to_broadcast([P, G, P // G]), func=ACT.Copy, scale=centre[:, c : c + 1])
             zh = sbuf(f"zh_sb{c}", [P, PACK, P], F32)
             nc.scalar.copy(out=zh[:], in_=bank[:].rearrange("r (p j) -> r j p", j=PACK))
-            turned = ps.tile([P, PACK, P], F32, name="turned", tag="turned", bufs=2)
+            turned = ps.tile([P, PACK, P], F32, name=f"turned{c}", tag=f"zh{c - 1}")
             shift_flat = shift[:].rearrange("r g a -> r (g a)")
             for j in range(PACK):
                 nc.tensor.matmul(out=turned[:, j, :], lhsT=shift_flat, rhs=ident[:], start=(j == 0), stop=False, is_transpose=True)
@@ -121,22 +118,33 @@ def tile_attend_lrcentred_soft_kernel(tc, query, keys_words, keys_scales, tab_wo
             nc.vector.tensor_tensor(out=hw[:], in0=hv[:], in1=vs_col[:].unsqueeze(1).to_broadcast([P, P, PACK]), op=ALU.mult)
             return quantize(f"h{c}", hw, P)
 
-        turned0 = centre_chunk(0)
-        turned1 = centre_chunk(1)
+        layer = []
+        for c in range(2):
+            grouped = sbuf(f"w1_bf{c}", [P, P, PACK], BF16)
+            round_and_group(grouped[:], w1_raw[0][:, :, c * P : (c + 1) * P])
+            codes, scales = quantize(f"w1q{c}", grouped, P)
+            layer.append(layer_product(c, codes[:], scales[:]))
+        grouped = sbuf("w1_bf_late", [P, 2 * P, PACK], BF16)
+        round_and_group(grouped[:], w1_raw[1][:])
+
+        keys_bytes = gather("keys_bytes", keys_plane, U8)
+        late = reused.tile([P, 2 * P], U32, name="late", align_bytes=64, offset=0)
+        page_sums = reused.tile([P, CHUNKS * G], F32, name="page_sums", align_bytes=64, offset=T // 2)
+        turned = [centre_chunk(0)]
+        late_scales = sbuf("late_scales", [P, 2 * P], U8)
+        nc.vector.quantize_mx(out=late[:].bitcast(FP8X4), scales=late_scales[:], in_=grouped[:].rearrange("p c j -> p (c j)"))
+        for c in range(2):
+            layer.append(layer_product(2 + c, late[:, c * P : (c + 1) * P], late_scales[:, c * P : (c + 1) * P]))
+        turned.append(centre_chunk(1))
 
         keys_codes = gather("keys_codes", keys_pool, U16)
-        keys_bytes = gather("keys_bytes", keys_plane, U8)
-        q_codes, q_scales = quantize("q", round_and_group("q_bf", q_raw[:]), Q)
+        q_bf = sbuf("q_bf", [P, Q, PACK], BF16)
+        nc.gpsimd.tensor_scalar(out=q_bf[:], in0=q_raw[:].rearrange("p j q -> p q j"), scalar1=1.0, scalar2=0.0, op0=ALU.mult, op1=ALU.add)
+        q_codes, q_scales = quantize("q", q_bf, Q)
         scores = ps.tile([P, I], F32, name="scores", tag="scores")
         nc.tensor.matmul_mx(out=scores[:], lhsT=q_codes[:].bitcast(FP8X4), lhsT_scale=q_scales[:], rhs=keys_codes[:].bitcast(FP4X4), rhs_scale=keys_bytes[:], start=True, stop=True)
-
-        hq = [finish_chunk(0, turned0)]
-        turned2 = centre_chunk(2)
         neg_max = sbuf("neg_max", [P, 1], F32)
         nc.vector.tensor_reduce(out=neg_max[:], in_=scores[:], axis=AXIS.X, op=ALU.max, negate=True)
-        hq.append(finish_chunk(1, turned1))
-        turned3 = centre_chunk(3)
-
         expo = sbuf("expo", [P, PACK, P], F32)
         row_sum = sbuf("row_sum", [P, 1], F32)
         nc.scalar.activation(out=expo[:], in_=scores[:].rearrange("q (p j) -> q j p", j=PACK), func=ACT.Exp, bias=neg_max[:], accum_out=row_sum[:])
@@ -147,15 +155,14 @@ def tile_attend_lrcentred_soft_kernel(tc, query, keys_words, keys_scales, tab_wo
         w_turned = ps.tile([P, PACK, Q], F32, name="w_turned", tag="w_turned")
         for j in range(PACK):
             nc.tensor.transpose(w_turned[:, j, :], weights[:, j, :], ident[:])
-        hq.append(finish_chunk(2, turned2))
         wt = sbuf("wt", [P, Q, PACK], BF16)
         nc.vector.tensor_tensor(out=wt[:], in0=w_turned[:].rearrange("p j q -> p q j"), in1=os_col[:].unsqueeze(1).to_broadcast([P, Q, PACK]), op=ALU.mult)
         w_codes, w_scales = quantize("w", wt, Q)
-        hq.append(finish_chunk(3, turned3))
 
+        turned.extend(centre_chunk(c) for c in range(2, CHUNKS))
         for c in range(CHUNKS):
-            codes, scales = hq[c]
-            acc = ps.tile([P, P], F32, name=f"acc{c}", tag=f"zh{c}")
+            codes, scales = finish_chunk(c, turned[c])
+            acc = ps.tile([P, P], F32, name=f"acc{c}", tag=f"zh{c - 1}")
             nc.tensor.matmul_mx(out=acc[:], lhsT=w_codes[:].bitcast(FP8X4), lhsT_scale=w_scales[:], rhs=codes[:].bitcast(FP8X4), rhs_scale=scales[:], start=True, stop=True)
             result = sbuf(f"result{c}", [P, P], F32)
             nc.scalar.copy(out=result[:], in_=acc[:])

from contextlib import ExitStack

import concourse.mybir as mybir
from concourse.masks import make_identity

D, K, R, T, I, Q, G = 512, 512, 512, 2048, 512, 128, 32
FLOPS = 2 * (D * Q * I + K * R * I + I * Q * R)

F32 = mybir.dt.float32
BF16 = mybir.dt.bfloat16
I32 = mybir.dt.int32
U32 = mybir.dt.uint32
U16 = mybir.dt.uint16
U8 = mybir.dt.uint8
FP8X4 = mybir.dt.float8_e4m3fn_x4
FP4X4 = mybir.dt.float4_e2m1fn_x4
ALU = mybir.AluOpType
ACT = mybir.ActivationFunctionType
AXIS = mybir.AxisListType

P = 128
PACK = 4
PAGE = I // G
CHUNKS = R // P


def tile_attend_lrcentred_soft_kernel(tc, query, keys_words, keys_scales, tab_words, tab_scales, w1, share, slot_factor, value_scale, offs, out):
    nc = tc.nc
    with ExitStack() as ctx:
        sb = ctx.enter_context(tc.tile_pool(name="sb", bufs=1))
        reused = ctx.enter_context(tc.tile_pool(name="reused", bufs=1))
        ps = ctx.enter_context(tc.psum_pool(name="ps", bufs=1))

        def sbuf(name, shape, dtype, tag=None):
            return sb.tile(shape, dtype, name=name, tag=tag or name, align_bytes=64)

        def load_scale_rows(queue, plane, rows):
            for quad in range(4):
                queue.dma_start(out=plane[32 * quad : 32 * quad + 4, :].bitcast(I32), in_=rows[0, 4 * quad : 4 * quad + 4, :].bitcast(I32))

        def gather(name, window, dtype):
            picked = sbuf(name, [P, I], dtype)
            nc.vector.tensor_copy(out=picked[:], in_=window[:].indirect(offsets[:]))
            return picked

        def quantize(name, grouped, width):
            codes = sbuf(name + "_codes", [P, width], U32)
            scales = sbuf(name + "_scales", [P, width], U8)
            nc.vector.quantize_mx(out=codes[:].bitcast(FP8X4), scales=scales[:], in_=grouped[:].rearrange("p c j -> p (c j)"))
            return codes, scales

        def round_and_group(grouped, rows):
            nc.scalar.activation(out=grouped.rearrange("p (c i) j -> p c j i", i=4), in_=rows.rearrange("p j (c i) -> p c j i", i=4), func=ACT.Copy)

        offsets = sb.tile([P, I // 16], U16, name="offsets")
        tab_plane = sbuf("tab_plane", [P, T], U8)
        keys_plane = reused.tile([P, T], U8, name="keys_plane", align_bytes=64, offset=0)
        nc.vector.memset(tab_plane[:].bitcast(I32), 0)
        nc.vector.memset(keys_plane[:].bitcast(I32), 0)

        nc.sync.dma_start(offsets[:], offs)
        tab_pool = sbuf("tab_pool", [P, T], U16)
        nc.sync.dma_start(out=tab_pool[:].bitcast(I32), in_=tab_words[0].bitcast(I32))
        load_scale_rows(nc.sync, tab_plane, tab_scales)

        w1_rows = w1.rearrange("(p j) r -> p j r", j=PACK)
        w1_raw = [sbuf(f"w1_raw{h}", [P, PACK, R // 2], F32) for h in range(2)]
        keys_pool = sbuf("keys_pool", [P, T], U16)
        q_raw = sbuf("q_raw", [P, PACK, Q], F32)
        nc.sync.dma_start(out=w1_raw[0][:], in_=w1_rows[:, :, : R // 2])
        nc.sync.dma_start(out=w1_raw[1][:], in_=w1_rows[:, :, R // 2 :])
        load_scale_rows(nc.sync, keys_plane, keys_scales)
        nc.sync.dma_start(out=q_raw[:], in_=query.rearrange("(p j) q -> p j q", j=PACK))
        nc.sync.dma_start(out=keys_pool[:].bitcast(I32), in_=keys_words[0].bitcast(I32))

        share_rows = sbuf("share_rows", [P, P], F32)
        nc.gpsimd.memset(share_rows[:], 0.0)
        nc.scalar.dma_start(out=share_rows[:CHUNKS, :], in_=share.rearrange("(c p) o -> c (p o)", p=P))
        vs_col = sbuf("vs_col", [P, PACK], F32)
        os_col = sbuf("os_col", [P, PACK], F32)
        nc.sync.dma_start(out=vs_col[:], in_=value_scale.rearrange("o (p j) -> (o p) j", j=PACK))
        nc.sync.dma_start(out=os_col[:], in_=slot_factor.rearrange("o (p j) -> (o p) j", j=PACK))
        ident = sbuf("ident", [P, P], F32)
        make_identity(nc, ident[:])
        centre = sbuf("centre", [P, CHUNKS], F32)
        share_turned = ps.tile([P, P], F32, name="share_turned", tag="w_turned")
        nc.tensor.transpose(share_turned[:], share_rows[:], ident[:])
        nc.vector.tensor_scalar(out=centre[:], in0=share_turned[:, :CHUNKS], scalar1=-1.0 / PAGE, scalar2=None, op0=ALU.mult)

        tab_codes = gather("tab_codes", tab_pool, U16)
        tab_bytes = gather("tab_bytes", tab_plane, U8)

        def layer_product(c, codes, scales):
            bank = ps.tile([P, I], F32, name=f"zh{c}", tag=f"zh{c}")
            nc.tensor.matmul_mx(out=bank[:], lhsT=codes.bitcast(FP8X4), lhsT_scale=scales, rhs=tab_codes[:].bitcast(FP4X4), rhs_scale=tab_bytes[:], start=True, stop=True)
            return bank

        def centre_chunk(c):
            bank = layer[c]
            page_sum = page_sums[:, c * G : (c + 1) * G]
            nc.vector.tensor_reduce(out=page_sum, in_=bank[:].rearrange("r (g s) -> r g s", s=PAGE), axis=AXIS.X, op=ALU.add)
            shift = sbuf(f"shift{c}", [P, G, P // G], F32)
            nc.scalar.activation(out=shift[:], in_=page_sum.unsqueeze(2).to_broadcast([P, G, P // G]), func=ACT.Copy, scale=centre[:, c : c + 1])
            zh = sbuf(f"zh_sb{c}", [P, PACK, P], F32)
            nc.scalar.copy(out=zh[:], in_=bank[:].rearrange("r (p j) -> r j p", j=PACK))
            turned = ps.tile([P, PACK, P], F32, name=f"turned{c}", tag=f"zh{c - 1}")
            shift_flat = shift[:].rearrange("r g a -> r (g a)")
            for j in range(PACK):
                nc.tensor.matmul(out=turned[:, j, :], lhsT=shift_flat, rhs=ident[:], start=(j == 0), stop=False, is_transpose=True)
            for j in range(PACK):
                nc.tensor.matmul(out=turned[:, j, :], lhsT=zh[:, j, :], rhs=ident[:], start=False, stop=(j == PACK - 1), is_transpose=True)
            return turned

        def finish_chunk(c, turned):
            hv = sbuf(f"hv{c}", [P, P, PACK], F32)
            nc.scalar.activation(out=hv[:], in_=turned[:].rearrange("p j r -> p r j"), func=ACT.Tanh)
            hw = sbuf(f"hw{c}", [P, P, PACK], BF16)
            nc.vector.tensor_tensor(out=hw[:], in0=hv[:], in1=vs_col[:].unsqueeze(1).to_broadcast([P, P, PACK]), op=ALU.mult)
            return quantize(f"h{c}", hw, P)

        layer = []
        for c in range(2):
            grouped = sbuf(f"w1_bf{c}", [P, P, PACK], BF16)
            round_and_group(grouped[:], w1_raw[0][:, :, c * P : (c + 1) * P])
            codes, scales = quantize(f"w1q{c}", grouped, P)
            layer.append(layer_product(c, codes[:], scales[:]))
        grouped = sbuf("w1_bf_late", [P, 2 * P, PACK], BF16)
        round_and_group(grouped[:], w1_raw[1][:])

        keys_bytes = gather("keys_bytes", keys_plane, U8)
        late = reused.tile([P, 2 * P], U32, name="late", align_bytes=64, offset=0)
        page_sums = reused.tile([P, CHUNKS * G], F32, name="page_sums", align_bytes=64, offset=T // 2)
        turned = [centre_chunk(0)]
        late_scales = sbuf("late_scales", [P, 2 * P], U8)
        nc.vector.quantize_mx(out=late[:].bitcast(FP8X4), scales=late_scales[:], in_=grouped[:].rearrange("p c j -> p (c j)"))
        for c in range(2):
            layer.append(layer_product(2 + c, late[:, c * P : (c + 1) * P], late_scales[:, c * P : (c + 1) * P]))
        turned.append(centre_chunk(1))

        keys_codes = gather("keys_codes", keys_pool, U16)
        q_bf = sbuf("q_bf", [P, Q, PACK], BF16)
        nc.gpsimd.tensor_scalar(out=q_bf[:], in0=q_raw[:].rearrange("p j q -> p q j"), scalar1=1.0, scalar2=0.0, op0=ALU.mult, op1=ALU.add)
        q_codes, q_scales = quantize("q", q_bf, Q)
        scores = ps.tile([P, I], F32, name="scores", tag="scores")
        nc.tensor.matmul_mx(out=scores[:], lhsT=q_codes[:].bitcast(FP8X4), lhsT_scale=q_scales[:], rhs=keys_codes[:].bitcast(FP4X4), rhs_scale=keys_bytes[:], start=True, stop=True)
        neg_max = sbuf("neg_max", [P, 1], F32)
        nc.vector.tensor_reduce(out=neg_max[:], in_=scores[:], axis=AXIS.X, op=ALU.max, negate=True)
        expo = sbuf("expo", [P, PACK, P], F32)
        row_sum = sbuf("row_sum", [P, 1], F32)
        nc.scalar.activation(out=expo[:], in_=scores[:].rearrange("q (p j) -> q j p", j=PACK), func=ACT.Exp, bias=neg_max[:], accum_out=row_sum[:])
        inv_sum = sbuf("inv_sum", [P, 1], F32)
        nc.vector.reciprocal(out=inv_sum[:], in_=row_sum[:])
        weights = sbuf("weights", [P, PACK, P], F32)
        nc.scalar.activation(out=weights[:], in_=expo[:], func=ACT.Copy, scale=inv_sum[:])
        w_turned = ps.tile([P, PACK, Q], F32, name="w_turned", tag="w_turned")
        for j in range(PACK):
            nc.tensor.transpose(w_turned[:, j, :], weights[:, j, :], ident[:])
        wt = sbuf("wt", [P, Q, PACK], BF16)
        nc.vector.tensor_tensor(out=wt[:], in0=w_turned[:].rearrange("p j q -> p q j"), in1=os_col[:].unsqueeze(1).to_broadcast([P, Q, PACK]), op=ALU.mult)
        w_codes, w_scales = quantize("w", wt, Q)

        turned.extend(centre_chunk(c) for c in range(2, CHUNKS))
        for c in range(CHUNKS):
            codes, scales = finish_chunk(c, turned[c])
            acc = ps.tile([P, P], F32, name=f"acc{c}", tag=f"zh{c - 1}")
            nc.tensor.matmul_mx(out=acc[:], lhsT=w_codes[:].bitcast(FP8X4), lhsT_scale=w_scales[:], rhs=codes[:].bitcast(FP8X4), rhs_scale=scales[:], start=True, stop=True)
            result = sbuf(f"result{c}", [P, P], F32)
            nc.scalar.copy(out=result[:], in_=acc[:])
            nc.sync.dma_start(out=out[:, c * P : (c + 1) * P], in_=result[:])
